import numpy as np
import ml_dtypes


def mxq(x, axis, fmt="e4m3"):
    dtype, down = {"e4m3": (ml_dtypes.float8_e4m3fn, 7), "e5m2": (ml_dtypes.float8_e5m2, 14)}[fmt]
    v = np.moveaxis(np.asarray(x, np.float32).astype(ml_dtypes.bfloat16).astype(np.float64), axis, -1)
    blocks = v.reshape(v.shape[:-1] + (-1, 32))
    amax = np.abs(blocks).max(-1, keepdims=True)
    byte = np.maximum(np.where(amax > 0, np.frexp(amax)[1] - 1 + 127, 0) - down, 1)
    scale = np.exp2(byte - 127.0)
    codes = (blocks / scale).astype(np.float32).astype(dtype).astype(np.float64)
    return np.moveaxis((codes * scale).reshape(v.shape), -1, axis)


WIDE = False


def mx_kscale(k):
    if not WIDE:
        return np.ones(k)
    levels = np.array([10, -10, 5, -5, 0])
    if k % 512:
        return np.exp2(np.random.permutation(np.resize(levels, k // 32))).repeat(32)
    a = np.empty((k // 512, 16))
    for p in range(k // 512):
        a[p, :8] = np.random.permutation(np.resize(levels, 8))
        for g in range(8):
            far = levels[np.abs(levels - a[p, g]) >= 10]
            a[p, g + 8] = far[np.random.randint(len(far))]
    return np.exp2(a.ravel()).repeat(32)


def f64(x):
    return np.asarray(x).astype(np.float64)


def striped(idx):
    return np.tile(np.asarray(idx).reshape(-1, 16).T, (8, 1)).astype(np.uint16)


def unstriped(offs):
    return offs[:16].T.reshape(-1).astype(np.int64)


E2M1 = np.array([0.0, 0.5, 1.0, 1.5, 2.0, 3.0, 4.0, 6.0, -0.0, -0.5, -1.0, -1.5, -2.0, -3.0, -4.0, -6.0])


def pack_weight(w, fmt):
    k, n = w.shape
    w = f64(np.asarray(w, np.float32).astype(ml_dtypes.bfloat16)).reshape(k // 32, 32, n)
    amax = np.abs(w).max(1)
    if fmt == "e4m3":
        byte = np.frexp(amax)[1] - 1 + 127 - 7
    else:
        mant, ex = np.frexp(amax / 6.0)
        byte = np.where(mant > 0.5, ex, ex - 1) + 127
    byte = np.clip(np.where(amax > 0, byte, 1), 1, 254)
    scaled = (w * np.exp2(127.0 - byte)[:, None, :]).reshape(k, n).astype(np.float32)
    by_word = np.ascontiguousarray(scaled.reshape(k // 512, 128, 4, n).transpose(0, 1, 3, 2))
    if fmt == "e4m3":
        words = by_word.astype(ml_dtypes.float8_e4m3fn).view(np.uint8)
    else:
        c = by_word.astype(ml_dtypes.float4_e2m1fn).view(np.uint8) & 0xF
        words = (c[..., 0::2] | (c[..., 1::2] << 4)).reshape(k // 512, 128, 2 * n)
    return np.ascontiguousarray(words), np.ascontiguousarray(byte.astype(np.uint8).reshape(k // 512, 16, n))


def unpack_weight(words, scales, fmt):
    g, _, n = scales.shape
    words = np.ascontiguousarray(words).reshape(g, 128, n, -1)
    if fmt == "e4m3":
        vals = words.view(ml_dtypes.float8_e4m3fn).astype(np.float64)
    else:
        nib = np.empty((g, 128, n, 4), np.uint8)
        nib[..., 0::2] = words & 0xF
        nib[..., 1::2] = words >> 4
        vals = E2M1[nib]
    vals = vals * np.repeat(np.exp2(scales.astype(np.float64) - 127.0), 8, axis=1)[..., None]
    return vals.transpose(0, 1, 3, 2).reshape(g * 512, n)


B, N, T, D, NQ = 1, 512, 2048, 512, 256
SEG = 8


def setup_inputs():
    n = np.random.standard_normal
    idx = np.random.permutation(T)[:B * N]
    s = mx_kscale(D)[:, None]
    kp = pack_weight(n((D, T)) / s, "e4m3")
    return {
        "qT": (n((B, D, NQ)) * s * (1.00 / np.sqrt(D))).astype(np.float32),
        "k_words": kp[0],
        "k_scales": kp[1],
        "kb": np.tile(n(2048), (128, 1)).astype(np.float32),
        "offs": striped(idx),
    }


def reference(qT, k_words, k_scales, kb, offs):
    idx = unstriped(offs)
    pick = lambda x, which: x[:, which].reshape(x.shape[0], B, -1).transpose(1, 0, 2)
    k = unpack_weight(k_words, k_scales, "e4m3")
    kg = pick(k, idx)
    qq = mxq(f64(qT), 1, "e4m3")
    a = qq.transpose(0, 2, 1) @ kg
    y = np.log(1.0 + np.maximum(a + pick(f64(kb), idx)[:, :1, :], 0.0)).reshape(B, NQ, N // SEG, SEG).max(-1)
    return y

@@ -1,0 +1,119 @@
+from contextlib import ExitStack
+
+import concourse.mybir as mybir
+from concourse.masks import make_identity
+
+N, T, D, NQ, SEG = 512, 2048, 512, 256, 8
+P = 128
+FLOPS = 2 * NQ * N * D
+BYTES = D * NQ * 4 + T * D + T * D // 32 + T * 4 + P * N // 16 * 2 + NQ * N // SEG * 4
+
+F32 = mybir.dt.float32
+BF16 = mybir.dt.bfloat16
+I32 = mybir.dt.int32
+U32 = mybir.dt.uint32
+U16 = mybir.dt.uint16
+U8 = mybir.dt.uint8
+FP8X4 = mybir.dt.float8_e4m3fn_x4
+ACT = mybir.ActivationFunctionType
+ALU = mybir.AluOpType
+AX = mybir.AxisListType
+
+CHUNKS = N // P
+HALF = N // 2
+RUNS = P // SEG
+
+
+def tile_attend_splade_topk_kernel(tc, qT, k_words, k_scales, kb, offs, out):
+    nc = tc.nc
+    with ExitStack() as ctx:
+        sb = ctx.enter_context(tc.tile_pool(name="sb", bufs=1))
+        ps = ctx.enter_context(tc.psum_pool(name="ps", bufs=1))
+
+        offsets = sb.tile([P, N // 16], U16, name="offsets")
+        scale_win = sb.tile([P, T // 4], I32, name="scale_win", align_bytes=64)
+        bias_win = sb.tile([P, T], F32, name="bias_win", align_bytes=64)
+        word_win = sb.tile([P, T], I32, name="word_win", align_bytes=64)
+        q_raw = sb.tile([P, 4, NQ], F32, name="q_raw", align_bytes=64)
+        ident = sb.tile([P, P], F32, name="ident", align_bytes=64)
+        one = sb.tile([P, 1], F32, name="one")
+        warm = sb.tile([P, 1], F32, name="warm")
+
+        nc.vector.memset(scale_win[:], 0)
+        nc.vector.memset(bias_win[:], 0.0)
+        nc.vector.memset(one[:], 1.0)
+        nc.vector.memset(ident[:], 0.0)
+
+        nc.sync.dma_start(offsets[:], offs)
+        nc.sync.dma_start(out=q_raw[:], in_=qT[0].rearrange("(p t) q -> p t q", t=4))
+        nc.sync.dma_start(out=word_win[:], in_=k_words[0].rearrange("p n t -> p (n t)").bitcast(I32))
+        for quad in range(4):
+            nc.scalar.dma_start(
+                out=scale_win[32 * quad : 32 * quad + 4, :],
+                in_=k_scales[0, 4 * quad : 4 * quad + 4, :].bitcast(I32),
+            )
+        nc.scalar.dma_start(out=bias_win[0:1, :], in_=kb[0:1, :])
+        nc.scalar.activation(warm[:], one[:], ACT.Ln)
+        make_identity(nc, ident[:], nomemset=True)
+
+        k_scale = sb.tile([P, N], U8, name="k_scale", align_bytes=64)
+        nc.vector.tensor_copy(k_scale[:], scale_win[:].bitcast(U8).indirect(offsets[:]))
+        bias_row = sb.tile([P, N], F32, name="bias_row", align_bytes=64)
+        nc.vector.tensor_copy(bias_row[:], bias_win[:].indirect(offsets[:]))
+
+        q_bf = sb.tile([P, NQ, 4], BF16, name="q_bf", align_bytes=64)
+        nc.scalar.activation(q_bf[:], q_raw[:].rearrange("p t q -> p q t"), ACT.Copy)
+        q_code = sb.tile([P, NQ], U32, name="q_code", align_bytes=64)
+        q_scale = sb.tile([P, NQ], U8, name="q_scale", align_bytes=64)
+        nc.vector.quantize_mx(
+            out=q_code[:].bitcast(FP8X4), scales=q_scale[:], in_=q_bf[:].rearrange("p q t -> p (q t)")
+        )
+
+        bias_ps = ps.tile([P, CHUNKS, P], F32, name="bias_ps", tag="turn3")
+        for c in range(CHUNKS):
+            nc.tensor.transpose(bias_ps[:, c, :], bias_row[:, c * P : (c + 1) * P], ident[:])
+        bias_col = sb.tile([P, CHUNKS], F32, name="bias_col")
+        nc.scalar.activation(bias_col[:], bias_ps[:, :, 0], ACT.Copy)
+
+        scores = []
+        for h in range(2):
+            k_code = sb.tile([P, HALF], U32, name=f"k_code{h}", align_bytes=64)
+            cols = HALF // 16
+            nc.vector.tensor_copy(
+                k_code[:], word_win[:].bitcast(U32).indirect(offsets[:, h * cols : (h + 1) * cols])
+            )
+            for u in range(2):
+                c = 2 * h + u
+                score = ps.tile([P, NQ], F32, name=f"score{c}")
+                nc.tensor.matmul_mx(
+                    out=score[:],
+                    lhsT=k_code[:, u * P : (u + 1) * P].bitcast(FP8X4),
+                    lhsT_scale=k_scale[:, c * P : (c + 1) * P],
+                    rhs=q_code[:].bitcast(FP8X4),
+                    rhs_scale=q_scale[:],
+                    start=True,
+                    stop=True,
+                )
+                scores.append(score)
+
+        best = sb.tile([P, 2, N // SEG], F32, name="best", align_bytes=64)
+        for c in range(CHUNKS):
+            relu = sb.tile([P, 2, P], F32, name=f"relu{c}", align_bytes=64)
+            src = scores[c][:].rearrange("p (m j) -> p j m", j=2)
+            if c == 2:
+                nc.vector.tensor_scalar(relu[:], src, bias_col[:, c : c + 1], 0.0, ALU.add, ALU.max)
+            else:
+                nc.scalar.activation(relu[:], src, ACT.Relu, bias=bias_col[:, c : c + 1])
+            turned = ps.tile([P, 2, P], F32, name=f"turned{c}", tag=f"turn{c}")
+            for j in range(2):
+                nc.tensor.transpose(turned[:, j, :], relu[:, j, :], ident[:])
+            nc.vector.tensor_reduce(
+                best[:, :, c * RUNS : (c + 1) * RUNS],
+                turned[:].rearrange("p j (s e) -> p j s e", e=SEG),
+                AX.X,
+                ALU.max,
+            )
+
+        result = sb.tile([P, 2 * N // SEG], F32, name="result", align_bytes=64)
+        nc.scalar.activation(result[:], best[:].rearrange("p j s -> p (j s)"), ACT.Ln, bias=one[:])
+        nc.sync.dma_start(out=out[0].rearrange("(m j) s -> m (j s)", j=2), in_=result[:])

@@ -22,17 +22,19 @@ AX = mybir.AxisListType
 CHUNKS = N // P
 HALF = N // 2
 RUNS = P // SEG
+BIAS_ROW = 8
 
 
 def tile_attend_splade_topk_kernel(tc, qT, k_words, k_scales, kb, offs, out):
     nc = tc.nc
     with ExitStack() as ctx:
         sb = ctx.enter_context(tc.tile_pool(name="sb", bufs=1))
+        shared = ctx.enter_context(tc.tile_pool(name="shared", bufs=1))
         ps = ctx.enter_context(tc.psum_pool(name="ps", bufs=1))
 
         offsets = sb.tile([P, N // 16], U16, name="offsets")
         scale_win = sb.tile([P, T // 4], I32, name="scale_win", align_bytes=64)
-        bias_win = sb.tile([P, T], F32, name="bias_win", align_bytes=64)
+        bias_win = shared.tile([P, T], F32, name="bias_win", align_bytes=64, offset=0)
         word_win = sb.tile([P, T], I32, name="word_win", align_bytes=64)
         q_raw = sb.tile([P, 4, NQ], F32, name="q_raw", align_bytes=64)
         ident = sb.tile([P, P], F32, name="ident", align_bytes=64)
@@ -52,7 +54,7 @@ def tile_attend_splade_topk_kernel(tc, qT, k_words, k_scales, kb, offs, out):
                 out=scale_win[32 * quad : 32 * quad + 4, :],
                 in_=k_scales[0, 4 * quad : 4 * quad + 4, :].bitcast(I32),
             )
-        nc.scalar.dma_start(out=bias_win[0:1, :], in_=kb[0:1, :])
+        nc.scalar.dma_start(out=bias_win[BIAS_ROW : BIAS_ROW + 1, :], in_=kb[0:1, :])
         nc.scalar.activation(warm[:], one[:], ACT.Ln)
         make_identity(nc, ident[:], nomemset=True)
 
@@ -62,8 +64,12 @@ def tile_attend_splade_topk_kernel(tc, qT, k_words, k_scales, kb, offs, out):
         nc.vector.tensor_copy(bias_row[:], bias_win[:].indirect(offsets[:]))
 
         q_bf = sb.tile([P, NQ, 4], BF16, name="q_bf", align_bytes=64)
-        nc.scalar.activation(q_bf[:], q_raw[:].rearrange("p t q -> p q t"), ACT.Copy)
-        q_code = sb.tile([P, NQ], U32, name="q_code", align_bytes=64)
+        nc.scalar.activation(
+            q_bf[:].rearrange("p (c i) t -> p c t i", i=4),
+            q_raw[:].rearrange("p t (c i) -> p c t i", i=4),
+            ACT.Copy,
+        )
+        q_code = shared.tile([P, NQ], U32, name="q_code", align_bytes=64, offset=0)
         q_scale = sb.tile([P, NQ], U8, name="q_scale", align_bytes=64)
         nc.vector.quantize_mx(
             out=q_code[:].bitcast(FP8X4), scales=q_scale[:], in_=q_bf[:].rearrange("p q t -> p (q t)")
@@ -73,11 +79,11 @@ def tile_attend_splade_topk_kernel(tc, qT, k_words, k_scales, kb, offs, out):
         for c in range(CHUNKS):
             nc.tensor.transpose(bias_ps[:, c, :], bias_row[:, c * P : (c + 1) * P], ident[:])
         bias_col = sb.tile([P, CHUNKS], F32, name="bias_col")
-        nc.scalar.activation(bias_col[:], bias_ps[:, :, 0], ACT.Copy)
+        nc.scalar.activation(bias_col[:], bias_ps[:, :, BIAS_ROW], ACT.Copy)
 
         scores = []
         for h in range(2):
-            k_code = sb.tile([P, HALF], U32, name=f"k_code{h}", align_bytes=64)
+            k_code = shared.tile([P, HALF], U32, name=f"k_code{h}", align_bytes=64, offset=4 * (NQ + h * HALF))
             cols = HALF // 16
             nc.vector.tensor_copy(
                 k_code[:], word_win[:].bitcast(U32).indirect(offsets[:, h * cols : (h + 1) * cols])

@@ -1,7 +1,6 @@
 from contextlib import ExitStack
 
 import concourse.mybir as mybir
-from concourse.masks import make_identity
 
 N, T, D, NQ, SEG = 512, 2048, 512, 256, 8
 P = 128
@@ -19,10 +18,23 @@ ACT = mybir.ActivationFunctionType
 ALU = mybir.AluOpType
 AX = mybir.AxisListType
 
-CHUNKS = N // P
+PACK = 4
+WORD = 4
 HALF = N // 2
-RUNS = P // SEG
-BIAS_ROW = 8
+LIST_COLS = HALF // 16
+RUNS = HALF // SEG
+BIAS_ROW = P - 1
+PITCH = 12
+SCALE_SPLIT = 256
+BIAS_SPLIT = 1344
+
+BIAS_WIN_AT = 0
+Q_CODE_AT = BIAS_WIN_AT
+K_CODE_AT = Q_CODE_AT + WORD * NQ
+K_SCALE_AT = K_CODE_AT + WORD * N
+LATE_Q_AT = BIAS_WIN_AT + WORD * T
+WORD_WIN_AT = LATE_Q_AT + WORD * PACK * P
+ZEROS_AT = WORD_WIN_AT - WORD * P // 2
 
 
 def tile_attend_splade_topk_kernel(tc, qT, k_words, k_scales, kb, offs, out):
@@ -33,93 +45,133 @@ def tile_attend_splade_topk_kernel(tc, qT, k_words, k_scales, kb, offs, out):
         ps = ctx.enter_context(tc.psum_pool(name="ps", bufs=1))
 
         offsets = sb.tile([P, N // 16], U16, name="offsets")
-        scale_win = sb.tile([P, T // 4], I32, name="scale_win", align_bytes=64)
-        bias_win = shared.tile([P, T], F32, name="bias_win", align_bytes=64, offset=0)
-        word_win = sb.tile([P, T], I32, name="word_win", align_bytes=64)
-        q_raw = sb.tile([P, 4, NQ], F32, name="q_raw", align_bytes=64)
+        scale_win = sb.tile([P, T // WORD], I32, name="scale_win", align_bytes=64)
+        bias_win = shared.tile([P, T], F32, name="bias_win", align_bytes=64, offset=BIAS_WIN_AT)
+        zeros = shared.tile([P, P], F32, name="zeros", align_bytes=64, offset=ZEROS_AT)
+        q_raw0 = sb.tile([P, PACK, P], F32, name="q_raw0", align_bytes=64)
+        q_raw1 = shared.tile([P, PACK, P], F32, name="q_raw1", align_bytes=64, offset=LATE_Q_AT)
+        word_win = shared.tile([P, T], I32, name="word_win", align_bytes=64, offset=WORD_WIN_AT)
         ident = sb.tile([P, P], F32, name="ident", align_bytes=64)
         one = sb.tile([P, 1], F32, name="one")
-        warm = sb.tile([P, 1], F32, name="warm")
+        sums = sb.tile([P, 2, 2, RUNS, PITCH], F32, name="sums", align_bytes=64)
 
-        nc.vector.memset(scale_win[:], 0)
-        nc.vector.memset(bias_win[:], 0.0)
+        def zero_on_vector(window, columns, zero):
+            middle = columns // 2 + 1
+            nc.vector.memset(window[:, 0:middle], zero)
+            nc.vector.memset(window[:, middle:columns], zero)
+
+        nc.scalar.dma_start(out=bias_win[BIAS_ROW:P, :], in_=kb[0:1, :])
         nc.vector.memset(one[:], 1.0)
-        nc.vector.memset(ident[:], 0.0)
+        zero_on_vector(scale_win[:], SCALE_SPLIT, 0)
+        zero_on_vector(bias_win[0:BIAS_ROW, :], BIAS_SPLIT, 0.0)
+        nc.gpsimd.memset(zeros[:], 0.0)
+        nc.gpsimd.memset(scale_win[:, SCALE_SPLIT : T // WORD], 0)
+        nc.gpsimd.affine_select(
+            out=ident[:],
+            in_=zeros[:],
+            compare_op=ALU.not_equal,
+            fill=1.0,
+            base=0,
+            pattern=[[-1, P]],
+            channel_multiplier=1,
+        )
+        nc.gpsimd.memset(bias_win[0:BIAS_ROW, BIAS_SPLIT:T], 0.0)
+        nc.scalar.activation(
+            sums[:].rearrange("p j h r e -> p (j h r) e")[:, :, SEG],
+            one[:].to_broadcast([P, 2 * 2 * RUNS]),
+            ACT.Ln,
+        )
 
+        q_rows = qT[0].rearrange("(p t) q -> p t q", t=PACK)
         nc.sync.dma_start(offsets[:], offs)
-        nc.sync.dma_start(out=q_raw[:], in_=qT[0].rearrange("(p t) q -> p t q", t=4))
-        nc.sync.dma_start(out=word_win[:], in_=k_words[0].rearrange("p n t -> p (n t)").bitcast(I32))
+        nc.sync.dma_start(out=q_raw0[:], in_=q_rows[:, :, 0:P])
         for quad in range(4):
-            nc.scalar.dma_start(
+            nc.sync.dma_start(
                 out=scale_win[32 * quad : 32 * quad + 4, :],
                 in_=k_scales[0, 4 * quad : 4 * quad + 4, :].bitcast(I32),
             )
-        nc.scalar.dma_start(out=bias_win[BIAS_ROW : BIAS_ROW + 1, :], in_=kb[0:1, :])
-        nc.scalar.activation(warm[:], one[:], ACT.Ln)
-        make_identity(nc, ident[:], nomemset=True)
+        nc.sync.dma_start(out=word_win[:], in_=k_words[0].rearrange("p n t -> p (n t)").bitcast(I32))
+        nc.sync.dma_start(out=q_raw1[:], in_=q_rows[:, :, P:NQ])
 
-        k_scale = sb.tile([P, N], U8, name="k_scale", align_bytes=64)
-        nc.vector.tensor_copy(k_scale[:], scale_win[:].bitcast(U8).indirect(offsets[:]))
+        def listed(window, h):
+            return window.indirect(offsets[:, h * LIST_COLS : (h + 1) * LIST_COLS])
+
         bias_row = sb.tile([P, N], F32, name="bias_row", align_bytes=64)
-        nc.vector.tensor_copy(bias_row[:], bias_win[:].indirect(offsets[:]))
-
-        q_bf = sb.tile([P, NQ, 4], BF16, name="q_bf", align_bytes=64)
-        nc.scalar.activation(
-            q_bf[:].rearrange("p (c i) t -> p c t i", i=4),
-            q_raw[:].rearrange("p t (c i) -> p c t i", i=4),
-            ACT.Copy,
-        )
-        q_code = shared.tile([P, NQ], U32, name="q_code", align_bytes=64, offset=0)
-        q_scale = sb.tile([P, NQ], U8, name="q_scale", align_bytes=64)
-        nc.vector.quantize_mx(
-            out=q_code[:].bitcast(FP8X4), scales=q_scale[:], in_=q_bf[:].rearrange("p q t -> p (q t)")
-        )
-
-        bias_ps = ps.tile([P, CHUNKS, P], F32, name="bias_ps", tag="turn3")
-        for c in range(CHUNKS):
-            nc.tensor.transpose(bias_ps[:, c, :], bias_row[:, c * P : (c + 1) * P], ident[:])
-        bias_col = sb.tile([P, CHUNKS], F32, name="bias_col")
-        nc.scalar.activation(bias_col[:], bias_ps[:, :, BIAS_ROW], ACT.Copy)
-
-        scores = []
         for h in range(2):
-            k_code = shared.tile([P, HALF], U32, name=f"k_code{h}", align_bytes=64, offset=4 * (NQ + h * HALF))
-            cols = HALF // 16
-            nc.vector.tensor_copy(
-                k_code[:], word_win[:].bitcast(U32).indirect(offsets[:, h * cols : (h + 1) * cols])
+            nc.vector.tensor_copy(bias_row[:, h * HALF : (h + 1) * HALF], listed(bias_win[:], h))
+        k_scale = shared.tile([P, N], U8, name="k_scale", align_bytes=64, offset=K_SCALE_AT)
+        nc.vector.tensor_copy(k_scale[:], scale_win[:].bitcast(U8).indirect(offsets[:]))
+
+        def quantise_queries(j, q_raw):
+            q_bf = sb.tile([P, P, PACK], BF16, name=f"q_bf{j}", align_bytes=64)
+            nc.scalar.activation(
+                q_bf[:].rearrange("p (c i) t -> p c t i", i=4),
+                q_raw[:].rearrange("p t (c i) -> p c t i", i=4),
+                ACT.Copy,
             )
+            q_code = shared.tile([P, P], U32, name=f"q_code{j}", align_bytes=64, offset=Q_CODE_AT + WORD * j * P)
+            q_scale = sb.tile([P, P], U8, name=f"q_scale{j}", align_bytes=64)
+            nc.vector.quantize_mx(
+                out=q_code[:].bitcast(FP8X4), scales=q_scale[:], in_=q_bf[:].rearrange("p q t -> p (q t)")
+            )
+            return q_code, q_scale
+
+        queries = [quantise_queries(0, q_raw0)]
+
+        def spread_over_partitions(h):
+            col_ps = ps.tile([P, 2, P], F32, name=f"col_ps{h}")
             for u in range(2):
-                c = 2 * h + u
-                score = ps.tile([P, NQ], F32, name=f"score{c}")
+                first = h * HALF + u * P
+                nc.tensor.transpose(col_ps[:, u, :], bias_row[:, first : first + P], ident[:])
+            bias_col = sb.tile([P, 2], F32, name=f"bias_col{h}")
+            nc.scalar.activation(bias_col[:], col_ps[:, :, BIAS_ROW], ACT.Copy)
+            all_ps = ps.tile([P, 2, P], F32, name=f"all_ps{h}")
+            for u in range(2):
+                nc.tensor.transpose(all_ps[:, u, :], bias_col[:, u : u + 1].to_broadcast([P, P]), ident[:])
+            return all_ps
+
+        spread = [spread_over_partitions(h) for h in range(2)]
+
+        k_codes = []
+        for h in range(2):
+            k_code = shared.tile(
+                [P, HALF], U32, name=f"k_code{h}", align_bytes=64, offset=K_CODE_AT + WORD * h * HALF
+            )
+            nc.vector.tensor_copy(k_code[:], listed(word_win[:].bitcast(U32), h))
+            k_codes.append(k_code)
+        queries.append(quantise_queries(1, q_raw1))
+
+        bias_all = []
+        for h in range(2):
+            bias_half = shared.tile(
+                [P, HALF], F32, name=f"bias_all{h}", align_bytes=64, offset=LATE_Q_AT + WORD * h * HALF
+            )
+            nc.scalar.activation(bias_half[:], spread[h][:].rearrange("p u n -> p (u n)"), ACT.Copy)
+            bias_all.append(bias_half)
+
+        for j in range(2):
+            q_code, q_scale = queries[j]
+            for h in range(2):
+                score = ps.tile([P, HALF], F32, name=f"score{j}{h}")
                 nc.tensor.matmul_mx(
                     out=score[:],
-                    lhsT=k_code[:, u * P : (u + 1) * P].bitcast(FP8X4),
-                    lhsT_scale=k_scale[:, c * P : (c + 1) * P],
-                    rhs=q_code[:].bitcast(FP8X4),
-                    rhs_scale=q_scale[:],
+                    lhsT=q_code[:].bitcast(FP8X4),
+                    lhsT_scale=q_scale[:],
+                    rhs=k_codes[h][:].bitcast(FP8X4),
+                    rhs_scale=k_scale[:, h * HALF : (h + 1) * HALF],
                     start=True,
                     stop=True,
                 )
-                scores.append(score)
+                nc.vector.tensor_tensor(
+                    sums[:, j, h, :, 0:SEG],
+                    score[:].rearrange("p (r e) -> p r e", e=SEG),
+                    bias_all[h][:].rearrange("p (r e) -> p r e", e=SEG),
+                    ALU.add,
+                )
 
-        best = sb.tile([P, 2, N // SEG], F32, name="best", align_bytes=64)
-        for c in range(CHUNKS):
-            relu = sb.tile([P, 2, P], F32, name=f"relu{c}", align_bytes=64)
-            src = scores[c][:].rearrange("p (m j) -> p j m", j=2)
-            if c == 2:
-                nc.vector.tensor_scalar(relu[:], src, bias_col[:, c : c + 1], 0.0, ALU.add, ALU.max)
-            else:
-                nc.scalar.activation(relu[:], src, ACT.Relu, bias=bias_col[:, c : c + 1])
-            turned = ps.tile([P, 2, P], F32, name=f"turned{c}", tag=f"turn{c}")
-            for j in range(2):
-                nc.tensor.transpose(turned[:, j, :], relu[:, j, :], ident[:])
-            nc.vector.tensor_reduce(
-                best[:, :, c * RUNS : (c + 1) * RUNS],
-                turned[:].rearrange("p j (s e) -> p j s e", e=SEG),
-                AX.X,
-                ALU.max,
-            )
-
-        result = sb.tile([P, 2 * N // SEG], F32, name="result", align_bytes=64)
-        nc.scalar.activation(result[:], best[:].rearrange("p j s -> p (j s)"), ACT.Ln, bias=one[:])
-        nc.sync.dma_start(out=out[0].rearrange("(m j) s -> m (j s)", j=2), in_=result[:])
+        for j in range(2):
+            best = sb.tile([P, 2, RUNS], F32, name=f"best{j}", align_bytes=64)
+            result = sb.tile([P, 2, RUNS], F32, name=f"result{j}", align_bytes=64)
+            nc.vector.tensor_reduce(best[:], sums[:, j, :, :, 0 : SEG + 1], AX.X, ALU.max)
+            nc.scalar.activation(result[:], best[:], ACT.Ln, bias=one[:])
+            nc.sync.dma_start(out=out[0, j * P : (j + 1) * P, :], in_=result[:].rearrange("p h r -> p (h r)"))

from contextlib import ExitStack

import concourse.mybir as mybir

N, T, D, NQ, SEG = 512, 2048, 512, 256, 8
P = 128
FLOPS = 2 * NQ * N * D
BYTES = D * NQ * 4 + T * D + T * D // 32 + T * 4 + P * N // 16 * 2 + NQ * N // SEG * 4

F32 = mybir.dt.float32
BF16 = mybir.dt.bfloat16
I32 = mybir.dt.int32
U32 = mybir.dt.uint32
U16 = mybir.dt.uint16
U8 = mybir.dt.uint8
FP8X4 = mybir.dt.float8_e4m3fn_x4
ACT = mybir.ActivationFunctionType
ALU = mybir.AluOpType
AX = mybir.AxisListType

PACK = 4
WORD = 4
HALF = N // 2
LIST_COLS = HALF // 16
RUNS = HALF // SEG
BIAS_ROW = P - 1
PITCH = 12
SCALE_SPLIT = 256
BIAS_SPLIT = 1344

BIAS_WIN_AT = 0
Q_CODE_AT = BIAS_WIN_AT
K_CODE_AT = Q_CODE_AT + WORD * NQ
K_SCALE_AT = K_CODE_AT + WORD * N
LATE_Q_AT = BIAS_WIN_AT + WORD * T
WORD_WIN_AT = LATE_Q_AT + WORD * PACK * P
ZEROS_AT = WORD_WIN_AT - WORD * P // 2


def tile_attend_splade_topk_kernel(tc, qT, k_words, k_scales, kb, offs, out):
    nc = tc.nc
    with ExitStack() as ctx:
        sb = ctx.enter_context(tc.tile_pool(name="sb", bufs=1))
        shared = ctx.enter_context(tc.tile_pool(name="shared", bufs=1))
        ps = ctx.enter_context(tc.psum_pool(name="ps", bufs=1))

        offsets = sb.tile([P, N // 16], U16, name="offsets")
        scale_win = sb.tile([P, T // WORD], I32, name="scale_win", align_bytes=64)
        bias_win = shared.tile([P, T], F32, name="bias_win", align_bytes=64, offset=BIAS_WIN_AT)
        zeros = shared.tile([P, P], F32, name="zeros", align_bytes=64, offset=ZEROS_AT)
        q_raw0 = sb.tile([P, PACK, P], F32, name="q_raw0", align_bytes=64)
        q_raw1 = shared.tile([P, PACK, P], F32, name="q_raw1", align_bytes=64, offset=LATE_Q_AT)
        word_win = shared.tile([P, T], I32, name="word_win", align_bytes=64, offset=WORD_WIN_AT)
        ident = sb.tile([P, P], F32, name="ident", align_bytes=64)
        one = sb.tile([P, 1], F32, name="one")
        sums = sb.tile([P, 2, 2, RUNS, PITCH], F32, name="sums", align_bytes=64)

        def zero_on_vector(window, columns, zero):
            middle = columns // 2 + 1
            nc.vector.memset(window[:, 0:middle], zero)
            nc.vector.memset(window[:, middle:columns], zero)

        nc.scalar.dma_start(out=bias_win[BIAS_ROW:P, :], in_=kb[0:1, :])
        nc.vector.memset(one[:], 1.0)
        zero_on_vector(scale_win[:], SCALE_SPLIT, 0)
        zero_on_vector(bias_win[0:BIAS_ROW, :], BIAS_SPLIT, 0.0)
        nc.gpsimd.memset(zeros[:], 0.0)
        nc.gpsimd.memset(scale_win[:, SCALE_SPLIT : T // WORD], 0)
        nc.gpsimd.affine_select(
            out=ident[:],
            in_=zeros[:],
            compare_op=ALU.not_equal,
            fill=1.0,
            base=0,
            pattern=[[-1, P]],
            channel_multiplier=1,
        )
        nc.gpsimd.memset(bias_win[0:BIAS_ROW, BIAS_SPLIT:T], 0.0)
        nc.scalar.activation(
            sums[:].rearrange("p j h r e -> p (j h r) e")[:, :, SEG],
            one[:].to_broadcast([P, 2 * 2 * RUNS]),
            ACT.Ln,
        )

        q_rows = qT[0].rearrange("(p t) q -> p t q", t=PACK)
        nc.sync.dma_start(offsets[:], offs)
        nc.sync.dma_start(out=q_raw0[:], in_=q_rows[:, :, 0:P])
        for quad in range(4):
            nc.sync.dma_start(
                out=scale_win[32 * quad : 32 * quad + 4, :],
                in_=k_scales[0, 4 * quad : 4 * quad + 4, :].bitcast(I32),
            )
        nc.sync.dma_start(out=word_win[:], in_=k_words[0].rearrange("p n t -> p (n t)").bitcast(I32))
        nc.sync.dma_start(out=q_raw1[:], in_=q_rows[:, :, P:NQ])

        def listed(window, h):
            return window.indirect(offsets[:, h * LIST_COLS : (h + 1) * LIST_COLS])

        bias_row = sb.tile([P, N], F32, name="bias_row", align_bytes=64)
        for h in range(2):
            nc.vector.tensor_copy(bias_row[:, h * HALF : (h + 1) * HALF], listed(bias_win[:], h))
        k_scale = shared.tile([P, N], U8, name="k_scale", align_bytes=64, offset=K_SCALE_AT)
        nc.vector.tensor_copy(k_scale[:], scale_win[:].bitcast(U8).indirect(offsets[:]))

        def quantise_queries(j, q_raw):
            q_bf = sb.tile([P, P, PACK], BF16, name=f"q_bf{j}", align_bytes=64)
            nc.scalar.activation(
                q_bf[:].rearrange("p (c i) t -> p c t i", i=4),
                q_raw[:].rearrange("p t (c i) -> p c t i", i=4),
                ACT.Copy,
            )
            q_code = shared.tile([P, P], U32, name=f"q_code{j}", align_bytes=64, offset=Q_CODE_AT + WORD * j * P)
            q_scale = sb.tile([P, P], U8, name=f"q_scale{j}", align_bytes=64)
            nc.vector.quantize_mx(
                out=q_code[:].bitcast(FP8X4), scales=q_scale[:], in_=q_bf[:].rearrange("p q t -> p (q t)")
            )
            return q_code, q_scale

        queries = [quantise_queries(0, q_raw0)]

        def spread_over_partitions(h):
            col_ps = ps.tile([P, 2, P], F32, name=f"col_ps{h}")
            for u in range(2):
                first = h * HALF + u * P
                nc.tensor.transpose(col_ps[:, u, :], bias_row[:, first : first + P], ident[:])
            bias_col = sb.tile([P, 2], F32, name=f"bias_col{h}")
            nc.scalar.activation(bias_col[:], col_ps[:, :, BIAS_ROW], ACT.Copy)
            all_ps = ps.tile([P, 2, P], F32, name=f"all_ps{h}")
            for u in range(2):
                nc.tensor.transpose(all_ps[:, u, :], bias_col[:, u : u + 1].to_broadcast([P, P]), ident[:])
            return all_ps

        spread = [spread_over_partitions(h) for h in range(2)]

        k_codes = []
        for h in range(2):
            k_code = shared.tile(
                [P, HALF], U32, name=f"k_code{h}", align_bytes=64, offset=K_CODE_AT + WORD * h * HALF
            )
            nc.vector.tensor_copy(k_code[:], listed(word_win[:].bitcast(U32), h))
            k_codes.append(k_code)
        queries.append(quantise_queries(1, q_raw1))

        bias_all = []
        for h in range(2):
            bias_half = shared.tile(
                [P, HALF], F32, name=f"bias_all{h}", align_bytes=64, offset=LATE_Q_AT + WORD * h * HALF
            )
            nc.scalar.activation(bias_half[:], spread[h][:].rearrange("p u n -> p (u n)"), ACT.Copy)
            bias_all.append(bias_half)

        for j in range(2):
            q_code, q_scale = queries[j]
            for h in range(2):
                score = ps.tile([P, HALF], F32, name=f"score{j}{h}")
                nc.tensor.matmul_mx(
                    out=score[:],
                    lhsT=q_code[:].bitcast(FP8X4),
                    lhsT_scale=q_scale[:],
                    rhs=k_codes[h][:].bitcast(FP8X4),
                    rhs_scale=k_scale[:, h * HALF : (h + 1) * HALF],
                    start=True,
                    stop=True,
                )
                nc.vector.tensor_tensor(
                    sums[:, j, h, :, 0:SEG],
                    score[:].rearrange("p (r e) -> p r e", e=SEG),
                    bias_all[h][:].rearrange("p (r e) -> p r e", e=SEG),
                    ALU.add,
                )

        for j in range(2):
            best = sb.tile([P, 2, RUNS], F32, name=f"best{j}", align_bytes=64)
            result = sb.tile([P, 2, RUNS], F32, name=f"result{j}", align_bytes=64)
            nc.vector.tensor_reduce(best[:], sums[:, j, :, :, 0 : SEG + 1], AX.X, ALU.max)
            nc.scalar.activation(result[:], best[:], ACT.Ln, bias=one[:])
            nc.sync.dma_start(out=out[0, j * P : (j + 1) * P, :], in_=result[:].rearrange("p h r -> p (h r)"))
